import numpy as np
import ml_dtypes

BF16 = ml_dtypes.bfloat16


def bf(x):
    return np.asarray(x, np.float32).astype(BF16)


def f32(x):
    return np.asarray(x, np.float32)


def f64(x):
    return np.asarray(x).astype(np.float64)


def striped(idx):
    return np.tile(idx.reshape(-1, 16).T, (8, 1))


S, K, M, N, E, Q = 256, 256, 128, 512, 8, 64


def gelu_tanh(v):
    return 0.5 * v * (1.0 + np.tanh(np.sqrt(2.0 / np.pi) * (v + 0.044715 * v**3)))


def two_experts():
    first = np.random.permutation(S).reshape(E, S // E)
    return np.concatenate([np.random.permutation(np.concatenate([first[e], first[(e + 1) % E]])) for e in range(E)])


def setup_inputs():
    return {"table": bf(np.random.standard_normal((K, S))), "w": bf(np.random.standard_normal((E, K, M)) / np.sqrt(K)), "b": f32(0.5 * np.random.standard_normal((M, 1))), "offs": striped(two_experts())}


def reference(table, w, b, offs):
    idx = offs[:16].T.reshape(-1)
    x = f64(table)[:, idx]
    y = np.concatenate([f64(w)[e].T @ x[:, e * Q : (e + 1) * Q] for e in range(E)], axis=1)
    return gelu_tanh(y + f64(b))

@@ -1,0 +1,51 @@
+import concourse.mybir as mybir
+
+BF16, F32, U16 = mybir.dt.bfloat16, mybir.dt.float32, mybir.dt.uint16
+GELU_TANH = mybir.ActivationFunctionType.Gelu_apprx_tanh
+
+P = 128
+S = 256
+K = 256
+KB = K // P
+M = 128
+E = 8
+Q = 64
+N = E * Q
+QC = Q // 16
+
+FLOPS = 2 * K * M * N
+
+
+def tile_gather_matmul_kernel(tc, table, w, b, offs, out):
+    nc = tc.nc
+    with (
+        tc.tile_pool(name="held", bufs=1) as held,
+        tc.psum_pool(name="psum", bufs=1) as psum,
+    ):
+        offsets = held.tile([P, N // 16], U16, name="offsets")
+        nc.sync.dma_start(offsets[:], offs)
+
+        blocks = [held.tile([P, S], BF16, name="block%d" % kb) for kb in range(KB)]
+        for kb in range(KB):
+            nc.sync.dma_start(blocks[kb][:], table[kb * P : (kb + 1) * P, :])
+
+        bias = held.tile([P, 1], F32, name="bias")
+        nc.scalar.dma_start(bias[:], b)
+        weights = held.tile([P, E * KB, M], BF16, name="weights")
+        nc.scalar.dma_start(weights[:], w.rearrange("e (kb p) m -> p (e kb) m", p=P))
+
+        y = psum.tile([P, N], F32, name="y")
+        for e in range(E):
+            piece = offsets[:, e * QC : (e + 1) * QC]
+            for kb in range(KB):
+                nc.tensor.matmul(
+                    y[:, e * Q : (e + 1) * Q],
+                    weights[:, e * KB + kb, :],
+                    blocks[kb][:].indirect(piece),
+                    start=(kb == 0),
+                    stop=(kb == KB - 1),
+                )
+
+        result = held.tile([P, N], F32, name="result")
+        nc.scalar.activation(result[:], y[:], GELU_TANH, bias=bias[:, 0:1])
+        nc.sync.dma_start(out, result[:])

@@ -13,6 +13,10 @@ Q = 64
 N = E * Q
 QC = Q // 16
 
+G = 2
+ST = E // G
+WARM = 12
+
 FLOPS = 2 * K * M * N
 
 
@@ -26,26 +30,42 @@ def tile_gather_matmul_kernel(tc, table, w, b, offs, out):
         nc.sync.dma_start(offsets[:], offs)
 
         blocks = [held.tile([P, S], BF16, name="block%d" % kb) for kb in range(KB)]
+        table_by_block = table.rearrange("(p kb) s -> kb p s", kb=KB)
         for kb in range(KB):
-            nc.sync.dma_start(blocks[kb][:], table[kb * P : (kb + 1) * P, :])
+            nc.sync.dma_start(blocks[kb][:], table_by_block[kb])
+
+        weights = [held.tile([P, G, KB * M], BF16, name="weights%d" % s) for s in range(ST)]
+        for s in range(ST):
+            queue = nc.scalar if s % 2 == 0 else nc.sync
+            queue.dma_start(weights[s][:], w[s * G : (s + 1) * G].rearrange("e (p kb) m -> p e (kb m)", kb=KB))
 
         bias = held.tile([P, 1], F32, name="bias")
         nc.scalar.dma_start(bias[:], b)
-        weights = held.tile([P, E * KB, M], BF16, name="weights")
-        nc.scalar.dma_start(weights[:], w.rearrange("e (kb p) m -> p (e kb) m", p=P))
 
-        y = psum.tile([P, N], F32, name="y")
-        for e in range(E):
-            piece = offsets[:, e * QC : (e + 1) * QC]
-            for kb in range(KB):
-                nc.tensor.matmul(
-                    y[:, e * Q : (e + 1) * Q],
-                    weights[:, e * KB + kb, :],
-                    blocks[kb][:].indirect(piece),
-                    start=(kb == 0),
-                    stop=(kb == KB - 1),
-                )
+        zeros = held.tile([P, P], BF16, name="zeros")
+        nc.vector.memset(zeros[:], 0.0)
 
-        result = held.tile([P, N], F32, name="result")
-        nc.scalar.activation(result[:], y[:], GELU_TANH, bias=bias[:, 0:1])
-        nc.sync.dma_start(out, result[:])
+        unread_gelu = held.tile([P, 1], F32, name="unread_gelu")
+        nc.scalar.activation(unread_gelu[:], zeros[:, 0:1], GELU_TANH)
+
+        unread_product = psum.tile([P, P], F32, name="unread_product")
+        for i in range(WARM):
+            nc.tensor.matmul(unread_product[:], zeros[:], zeros[:], start=True, stop=True)
+
+        for s in range(ST):
+            y = psum.tile([P, G * Q], F32, name="y%d" % s)
+            for g in range(G):
+                e = s * G + g
+                piece = offsets[:, e * QC : (e + 1) * QC]
+                for kb in range(KB):
+                    nc.tensor.matmul(
+                        y[:, g * Q : (g + 1) * Q],
+                        weights[s][:, g, kb * M : (kb + 1) * M],
+                        blocks[kb][:].indirect(piece),
+                        start=(kb == 0),
+                        stop=(kb == KB - 1),
+                    )
+
+            result = held.tile([P, G * Q], F32, name="result%d" % s)
+            nc.scalar.activation(result[:], y[:], GELU_TANH, bias=bias[:, 0:1])
+            nc.sync.dma_start(out[:, s * G * Q : (s + 1) * G * Q], result[:])

@@ -15,7 +15,7 @@ QC = Q // 16
 
 G = 2
 ST = E // G
-WARM = 12
+WARM = 16
 
 FLOPS = 2 * K * M * N
 

@@ -32,12 +32,11 @@ def tile_gather_matmul_kernel(tc, table, w, b, offs, out):
         blocks = [held.tile([P, S], BF16, name="block%d" % kb) for kb in range(KB)]
         table_by_block = table.rearrange("(p kb) s -> kb p s", kb=KB)
         for kb in range(KB):
-            nc.sync.dma_start(blocks[kb][:], table_by_block[kb])
+            nc.scalar.dma_start(blocks[kb][:], table_by_block[kb])
 
         weights = [held.tile([P, G, KB * M], BF16, name="weights%d" % s) for s in range(ST)]
         for s in range(ST):
-            queue = nc.scalar if s % 2 == 0 else nc.sync
-            queue.dma_start(weights[s][:], w[s * G : (s + 1) * G].rearrange("e (p kb) m -> p e (kb m)", kb=KB))
+            nc.sync.dma_start(weights[s][:], w[s * G : (s + 1) * G].rearrange("e (p kb) m -> p e (kb m)", kb=KB))
 
         bias = held.tile([P, 1], F32, name="bias")
         nc.scalar.dma_start(bias[:], b)

@@ -15,6 +15,7 @@ QC = Q // 16
 
 G = 2
 ST = E // G
+ROW_ALIGN = 256
 WARM = 16
 
 FLOPS = 2 * K * M * N
@@ -29,12 +30,12 @@ def tile_gather_matmul_kernel(tc, table, w, b, offs, out):
         offsets = held.tile([P, N // 16], U16, name="offsets")
         nc.sync.dma_start(offsets[:], offs)
 
-        blocks = [held.tile([P, S], BF16, name="block%d" % kb) for kb in range(KB)]
+        blocks = [held.tile([P, S], BF16, name="block%d" % kb, align_bytes=ROW_ALIGN) for kb in range(KB)]
         table_by_block = table.rearrange("(p kb) s -> kb p s", kb=KB)
         for kb in range(KB):
             nc.scalar.dma_start(blocks[kb][:], table_by_block[kb])
 
-        weights = [held.tile([P, G, KB * M], BF16, name="weights%d" % s) for s in range(ST)]
+        weights = [held.tile([P, G, KB * M], BF16, name="weights%d" % s, align_bytes=ROW_ALIGN) for s in range(ST)]
         for s in range(ST):
             nc.sync.dma_start(weights[s][:], w[s * G : (s + 1) * G].rearrange("e (p kb) m -> p e (kb m)", kb=KB))
 
@@ -65,6 +66,6 @@ def tile_gather_matmul_kernel(tc, table, w, b, offs, out):
                         stop=(kb == KB - 1),
                     )
 
-            result = held.tile([P, G * Q], F32, name="result%d" % s)
+            result = held.tile([P, G * Q], F32, name="result%d" % s, align_bytes=ROW_ALIGN)
             nc.scalar.activation(result[:], y[:], GELU_TANH, bias=bias[:, 0:1])
             nc.sync.dma_start(out[:, s * G * Q : (s + 1) * G * Q], result[:])

@@ -30,6 +30,9 @@ def tile_gather_matmul_kernel(tc, table, w, b, offs, out):
         offsets = held.tile([P, N // 16], U16, name="offsets")
         nc.sync.dma_start(offsets[:], offs)
 
+        bias = held.tile([P, 1], F32, name="bias")
+        nc.sync.dma_start(bias[:], b)
+
         blocks = [held.tile([P, S], BF16, name="block%d" % kb, align_bytes=ROW_ALIGN) for kb in range(KB)]
         table_by_block = table.rearrange("(p kb) s -> kb p s", kb=KB)
         for kb in range(KB):
@@ -38,9 +41,6 @@ def tile_gather_matmul_kernel(tc, table, w, b, offs, out):
         weights = [held.tile([P, G, KB * M], BF16, name="weights%d" % s, align_bytes=ROW_ALIGN) for s in range(ST)]
         for s in range(ST):
             nc.sync.dma_start(weights[s][:], w[s * G : (s + 1) * G].rearrange("e (p kb) m -> p e (kb m)", kb=KB))
-
-        bias = held.tile([P, 1], F32, name="bias")
-        nc.scalar.dma_start(bias[:], b)
 
         zeros = held.tile([P, P], BF16, name="zeros")
         nc.vector.memset(zeros[:], 0.0)

@@ -14,7 +14,8 @@ N = E * Q
 QC = Q // 16
 
 G = 2
-ST = E // G
+STAGE_EXPERTS = (2, 2, 2, 1, 1)
+assert sum(STAGE_EXPERTS) == E
 ROW_ALIGN = 256
 WARM = 16
 
@@ -38,9 +39,9 @@ def tile_gather_matmul_kernel(tc, table, w, b, offs, out):
         for kb in range(KB):
             nc.scalar.dma_start(blocks[kb][:], table_by_block[kb])
 
-        weights = [held.tile([P, G, KB * M], BF16, name="weights%d" % s, align_bytes=ROW_ALIGN) for s in range(ST)]
-        for s in range(ST):
-            nc.sync.dma_start(weights[s][:], w[s * G : (s + 1) * G].rearrange("e (p kb) m -> p e (kb m)", kb=KB))
+        weights = [held.tile([P, G, KB * M], BF16, name="weights%d" % l, align_bytes=ROW_ALIGN) for l in range(E // G)]
+        for l in range(E // G):
+            nc.sync.dma_start(weights[l][:], w[l * G : (l + 1) * G].rearrange("e (p kb) m -> p e (kb m)", kb=KB))
 
         zeros = held.tile([P, P], BF16, name="zeros")
         nc.vector.memset(zeros[:], 0.0)
@@ -52,20 +53,26 @@ def tile_gather_matmul_kernel(tc, table, w, b, offs, out):
         for i in range(WARM):
             nc.tensor.matmul(unread_product[:], zeros[:], zeros[:], start=True, stop=True)
 
-        for s in range(ST):
-            y = psum.tile([P, G * Q], F32, name="y%d" % s)
-            for g in range(G):
-                e = s * G + g
+        results = [held.tile([P, G * Q], F32, name="result%d" % l, align_bytes=ROW_ALIGN) for l in range(E // G)]
+
+        first = 0
+        for s, count in enumerate(STAGE_EXPERTS):
+            y = psum.tile([P, count * Q], F32, name="y%d" % s)
+            for g in range(count):
+                e = first + g
                 piece = offsets[:, e * QC : (e + 1) * QC]
                 for kb in range(KB):
                     nc.tensor.matmul(
                         y[:, g * Q : (g + 1) * Q],
-                        weights[s][:, g, kb * M : (kb + 1) * M],
+                        weights[e // G][:, e % G, kb * M : (kb + 1) * M],
                         blocks[kb][:].indirect(piece),
                         start=(kb == 0),
                         stop=(kb == KB - 1),
                     )
 
-            result = held.tile([P, G * Q], F32, name="result%d" % s, align_bytes=ROW_ALIGN)
-            nc.scalar.activation(result[:], y[:], GELU_TANH, bias=bias[:, 0:1])
-            nc.sync.dma_start(out[:, s * G * Q : (s + 1) * G * Q], result[:])
+            l = first // G
+            column = (first % G) * Q
+            nc.scalar.activation(results[l][:, column : column + count * Q], y[:], GELU_TANH, bias=bias[:, 0:1])
+            first += count
+            if first % G == 0:
+                nc.sync.dma_start(out[:, l * G * Q : (l + 1) * G * Q], results[l][:])

@@ -31,17 +31,18 @@ def tile_gather_matmul_kernel(tc, table, w, b, offs, out):
         offsets = held.tile([P, N // 16], U16, name="offsets")
         nc.sync.dma_start(offsets[:], offs)
 
+        tokens = held.tile([P, KB, S], BF16, name="tokens", align_bytes=ROW_ALIGN)
+        nc.scalar.dma_start(tokens[:], table.rearrange("(p kb) s -> p kb s", kb=KB))
+
         bias = held.tile([P, 1], F32, name="bias")
-        nc.sync.dma_start(bias[:], b)
+        nc.scalar.dma_start(bias[:], b)
 
-        blocks = [held.tile([P, S], BF16, name="block%d" % kb, align_bytes=ROW_ALIGN) for kb in range(KB)]
-        table_by_block = table.rearrange("(p kb) s -> kb p s", kb=KB)
-        for kb in range(KB):
-            nc.scalar.dma_start(blocks[kb][:], table_by_block[kb])
-
-        weights = [held.tile([P, G, KB * M], BF16, name="weights%d" % l, align_bytes=ROW_ALIGN) for l in range(E // G)]
-        for l in range(E // G):
-            nc.sync.dma_start(weights[l][:], w[l * G : (l + 1) * G].rearrange("e (p kb) m -> p e (kb m)", kb=KB))
+        weights = []
+        first = 0
+        for s, count in enumerate(STAGE_EXPERTS):
+            weights.append(held.tile([P, count, KB * M], BF16, name="weights%d" % s, align_bytes=ROW_ALIGN))
+            nc.sync.dma_start(weights[s][:], w[first : first + count].rearrange("e (p kb) m -> p e (kb m)", kb=KB))
+            first += count
 
         zeros = held.tile([P, P], BF16, name="zeros")
         nc.vector.memset(zeros[:], 0.0)
@@ -64,8 +65,8 @@ def tile_gather_matmul_kernel(tc, table, w, b, offs, out):
                 for kb in range(KB):
                     nc.tensor.matmul(
                         y[:, g * Q : (g + 1) * Q],
-                        weights[e // G][:, e % G, kb * M : (kb + 1) * M],
-                        blocks[kb][:].indirect(piece),
+                        weights[s][:, g, kb * M : (kb + 1) * M],
+                        tokens[:, kb, :].indirect(piece),
                         start=(kb == 0),
                         stop=(kb == KB - 1),
                     )

@@ -44,15 +44,16 @@ def tile_gather_matmul_kernel(tc, table, w, b, offs, out):
             nc.sync.dma_start(weights[s][:], w[first : first + count].rearrange("e (p kb) m -> p e (kb m)", kb=KB))
             first += count
 
-        zeros = held.tile([P, P], BF16, name="zeros")
+        zeros = held.tile([P, 1], BF16, name="zeros")
         nc.vector.memset(zeros[:], 0.0)
+        many_zeros = zeros[:].to_broadcast([P, P])
 
         unread_gelu = held.tile([P, 1], F32, name="unread_gelu")
-        nc.scalar.activation(unread_gelu[:], zeros[:, 0:1], GELU_TANH)
+        nc.scalar.activation(unread_gelu[:], zeros[:], GELU_TANH)
 
         unread_product = psum.tile([P, P], F32, name="unread_product")
         for i in range(WARM):
-            nc.tensor.matmul(unread_product[:], zeros[:], zeros[:], start=True, stop=True)
+            nc.tensor.matmul(unread_product[:], many_zeros, many_zeros, start=True, stop=True)
 
         results = [held.tile([P, G * Q], F32, name="result%d" % l, align_bytes=ROW_ALIGN) for l in range(E // G)]
 

@@ -32,17 +32,17 @@ def tile_gather_matmul_kernel(tc, table, w, b, offs, out):
         nc.sync.dma_start(offsets[:], offs)
 
         tokens = held.tile([P, KB, S], BF16, name="tokens", align_bytes=ROW_ALIGN)
-        nc.scalar.dma_start(tokens[:], table.rearrange("(p kb) s -> p kb s", kb=KB))
+        nc.sync.dma_start(tokens[:], table.rearrange("(p kb) s -> p kb s", kb=KB))
 
         bias = held.tile([P, 1], F32, name="bias")
-        nc.scalar.dma_start(bias[:], b)
-
         weights = []
         first = 0
         for s, count in enumerate(STAGE_EXPERTS):
             weights.append(held.tile([P, count, KB * M], BF16, name="weights%d" % s, align_bytes=ROW_ALIGN))
             nc.sync.dma_start(weights[s][:], w[first : first + count].rearrange("e (p kb) m -> p e (kb m)", kb=KB))
             first += count
+            if s == 0:
+                nc.sync.dma_start(bias[:], b)
 
         zeros = held.tile([P, 1], BF16, name="zeros")
         nc.vector.memset(zeros[:], 0.0)

@@ -16,6 +16,7 @@ QC = Q // 16
 G = 2
 STAGE_EXPERTS = (2, 2, 2, 1, 1)
 assert sum(STAGE_EXPERTS) == E
+SQ = 32
 ROW_ALIGN = 256
 WARM = 16
 
@@ -34,19 +35,20 @@ def tile_gather_matmul_kernel(tc, table, w, b, offs, out):
         tokens = held.tile([P, KB, S], BF16, name="tokens", align_bytes=ROW_ALIGN)
         nc.sync.dma_start(tokens[:], table.rearrange("(p kb) s -> p kb s", kb=KB))
 
-        bias = held.tile([P, 1], F32, name="bias")
-        weights = []
-        first = 0
-        for s, count in enumerate(STAGE_EXPERTS):
-            weights.append(held.tile([P, count, KB * M], BF16, name="weights%d" % s, align_bytes=ROW_ALIGN))
-            nc.sync.dma_start(weights[s][:], w[first : first + count].rearrange("e (p kb) m -> p e (kb m)", kb=KB))
-            first += count
-            if s == 0:
-                nc.sync.dma_start(bias[:], b)
+        weights = [held.tile([P, G, KB * M], BF16, name="weights%d" % l, align_bytes=ROW_ALIGN) for l in range(E // G)]
+        for l in range(E // G):
+            nc.sync.dma_start(weights[l][:], w[l * G : (l + 1) * G].rearrange("e (p kb) m -> p e (kb m)", kb=KB))
 
         zeros = held.tile([P, 1], BF16, name="zeros")
         nc.vector.memset(zeros[:], 0.0)
         many_zeros = zeros[:].to_broadcast([P, P])
+
+        bias_rows = held.tile([P, SQ], F32, name="bias_rows", align_bytes=ROW_ALIGN)
+        nc.vector.memset(bias_rows[:], 0.0)
+        nc.scalar.dma_start(bias_rows[::SQ, :], b.rearrange("(q f) o -> q (f o)", f=SQ))
+        bias_columns = held.tile([P, SQ], F32, name="bias_columns", align_bytes=ROW_ALIGN)
+        nc.vector.transpose(bias_columns[:], bias_rows[:])
+        bias = bias_columns[:, 0:1]
 
         unread_gelu = held.tile([P, 1], F32, name="unread_gelu")
         nc.scalar.activation(unread_gelu[:], zeros[:], GELU_TANH)
@@ -66,7 +68,7 @@ def tile_gather_matmul_kernel(tc, table, w, b, offs, out):
                 for kb in range(KB):
                     nc.tensor.matmul(
                         y[:, g * Q : (g + 1) * Q],
-                        weights[s][:, g, kb * M : (kb + 1) * M],
+                        weights[e // G][:, e % G, kb * M : (kb + 1) * M],
                         tokens[:, kb, :].indirect(piece),
                         start=(kb == 0),
                         stop=(kb == KB - 1),
@@ -74,7 +76,7 @@ def tile_gather_matmul_kernel(tc, table, w, b, offs, out):
 
             l = first // G
             column = (first % G) * Q
-            nc.scalar.activation(results[l][:, column : column + count * Q], y[:], GELU_TANH, bias=bias[:, 0:1])
+            nc.scalar.activation(results[l][:, column : column + count * Q], y[:], GELU_TANH, bias=bias)
             first += count
             if first % G == 0:
                 nc.sync.dma_start(out[:, l * G * Q : (l + 1) * G * Q], results[l][:])

@@ -18,7 +18,7 @@ STAGE_EXPERTS = (2, 2, 2, 1, 1)
 assert sum(STAGE_EXPERTS) == E
 SQ = 32
 ROW_ALIGN = 256
-WARM = 16
+WARM = 14
 
 FLOPS = 2 * K * M * N
 

@@ -14,11 +14,13 @@ N = E * Q
 QC = Q // 16
 
 G = 2
+LOAD_EXPERTS = (1, 2, 2, 3)
+assert sum(LOAD_EXPERTS) == E
 STAGE_EXPERTS = (2, 2, 2, 1, 1)
 assert sum(STAGE_EXPERTS) == E
 SQ = 32
 ROW_ALIGN = 256
-WARM = 14
+WARM = 12
 
 FLOPS = 2 * K * M * N
 
@@ -33,11 +35,15 @@ def tile_gather_matmul_kernel(tc, table, w, b, offs, out):
         nc.sync.dma_start(offsets[:], offs)
 
         tokens = held.tile([P, KB, S], BF16, name="tokens", align_bytes=ROW_ALIGN)
-        nc.sync.dma_start(tokens[:], table.rearrange("(p kb) s -> p kb s", kb=KB))
+        nc.scalar.dma_start(tokens[:], table.rearrange("(p kb) s -> p kb s", kb=KB))
 
-        weights = [held.tile([P, G, KB * M], BF16, name="weights%d" % l, align_bytes=ROW_ALIGN) for l in range(E // G)]
-        for l in range(E // G):
-            nc.sync.dma_start(weights[l][:], w[l * G : (l + 1) * G].rearrange("e (p kb) m -> p e (kb m)", kb=KB))
+        weights = []
+        for l, count in enumerate(LOAD_EXPERTS):
+            first = len(weights)
+            loaded = held.tile([P, count, KB * M], BF16, name="weights%d" % l, align_bytes=ROW_ALIGN)
+            queue = nc.sync if l == 0 else nc.scalar
+            queue.dma_start(loaded[:], w[first : first + count].rearrange("e (p kb) m -> p e (kb m)", kb=KB))
+            weights.extend([loaded[:, g, :] for g in range(count)])
 
         zeros = held.tile([P, 1], BF16, name="zeros")
         nc.vector.memset(zeros[:], 0.0)
@@ -45,7 +51,7 @@ def tile_gather_matmul_kernel(tc, table, w, b, offs, out):
 
         bias_rows = held.tile([P, SQ], F32, name="bias_rows", align_bytes=ROW_ALIGN)
         nc.vector.memset(bias_rows[:], 0.0)
-        nc.scalar.dma_start(bias_rows[::SQ, :], b.rearrange("(q f) o -> q (f o)", f=SQ))
+        nc.sync.dma_start(bias_rows[::SQ, :], b.rearrange("(q f) o -> q (f o)", f=SQ))
         bias_columns = held.tile([P, SQ], F32, name="bias_columns", align_bytes=ROW_ALIGN)
         nc.vector.transpose(bias_columns[:], bias_rows[:])
         bias = bias_columns[:, 0:1]
@@ -68,7 +74,7 @@ def tile_gather_matmul_kernel(tc, table, w, b, offs, out):
                 for kb in range(KB):
                     nc.tensor.matmul(
                         y[:, g * Q : (g + 1) * Q],
-                        weights[e // G][:, e % G, kb * M : (kb + 1) * M],
+                        weights[e][:, kb * M : (kb + 1) * M],
                         tokens[:, kb, :].indirect(piece),
                         start=(kb == 0),
                         stop=(kb == KB - 1),

@@ -14,7 +14,7 @@ N = E * Q
 QC = Q // 16
 
 G = 2
-LOAD_EXPERTS = (1, 2, 2, 3)
+LOAD_EXPERTS = (1, 2, 2, 2, 1)
 assert sum(LOAD_EXPERTS) == E
 STAGE_EXPERTS = (2, 2, 2, 1, 1)
 assert sum(STAGE_EXPERTS) == E

import concourse.mybir as mybir

BF16, F32, U16 = mybir.dt.bfloat16, mybir.dt.float32, mybir.dt.uint16
GELU_TANH = mybir.ActivationFunctionType.Gelu_apprx_tanh

P = 128
S = 256
K = 256
KB = K // P
M = 128
E = 8
Q = 64
N = E * Q
QC = Q // 16

G = 2
LOAD_EXPERTS = (1, 2, 2, 2, 1)
assert sum(LOAD_EXPERTS) == E
STAGE_EXPERTS = (2, 2, 2, 1, 1)
assert sum(STAGE_EXPERTS) == E
SQ = 32
ROW_ALIGN = 256
WARM = 12

FLOPS = 2 * K * M * N


def tile_gather_matmul_kernel(tc, table, w, b, offs, out):
    nc = tc.nc
    with (
        tc.tile_pool(name="held", bufs=1) as held,
        tc.psum_pool(name="psum", bufs=1) as psum,
    ):
        offsets = held.tile([P, N // 16], U16, name="offsets")
        nc.sync.dma_start(offsets[:], offs)

        tokens = held.tile([P, KB, S], BF16, name="tokens", align_bytes=ROW_ALIGN)
        nc.scalar.dma_start(tokens[:], table.rearrange("(p kb) s -> p kb s", kb=KB))

        weights = []
        for l, count in enumerate(LOAD_EXPERTS):
            first = len(weights)
            loaded = held.tile([P, count, KB * M], BF16, name="weights%d" % l, align_bytes=ROW_ALIGN)
            queue = nc.sync if l == 0 else nc.scalar
            queue.dma_start(loaded[:], w[first : first + count].rearrange("e (p kb) m -> p e (kb m)", kb=KB))
            weights.extend([loaded[:, g, :] for g in range(count)])

        zeros = held.tile([P, 1], BF16, name="zeros")
        nc.vector.memset(zeros[:], 0.0)
        many_zeros = zeros[:].to_broadcast([P, P])

        bias_rows = held.tile([P, SQ], F32, name="bias_rows", align_bytes=ROW_ALIGN)
        nc.vector.memset(bias_rows[:], 0.0)
        nc.sync.dma_start(bias_rows[::SQ, :], b.rearrange("(q f) o -> q (f o)", f=SQ))
        bias_columns = held.tile([P, SQ], F32, name="bias_columns", align_bytes=ROW_ALIGN)
        nc.vector.transpose(bias_columns[:], bias_rows[:])
        bias = bias_columns[:, 0:1]

        unread_gelu = held.tile([P, 1], F32, name="unread_gelu")
        nc.scalar.activation(unread_gelu[:], zeros[:], GELU_TANH)

        unread_product = psum.tile([P, P], F32, name="unread_product")
        for i in range(WARM):
            nc.tensor.matmul(unread_product[:], many_zeros, many_zeros, start=True, stop=True)

        results = [held.tile([P, G * Q], F32, name="result%d" % l, align_bytes=ROW_ALIGN) for l in range(E // G)]

        first = 0
        for s, count in enumerate(STAGE_EXPERTS):
            y = psum.tile([P, count * Q], F32, name="y%d" % s)
            for g in range(count):
                e = first + g
                piece = offsets[:, e * QC : (e + 1) * QC]
                for kb in range(KB):
                    nc.tensor.matmul(
                        y[:, g * Q : (g + 1) * Q],
                        weights[e][:, kb * M : (kb + 1) * M],
                        tokens[:, kb, :].indirect(piece),
                        start=(kb == 0),
                        stop=(kb == KB - 1),
                    )

            l = first // G
            column = (first % G) * Q
            nc.scalar.activation(results[l][:, column : column + count * Q], y[:], GELU_TANH, bias=bias)
            first += count
            if first % G == 0:
                nc.sync.dma_start(out[:, l * G * Q : (l + 1) * G * Q], results[l][:])
